import numpy as np, ml_dtypes
CORES = [4,20,60,84,92,100,116]
N = 7
import mx_ref
NC = 128
BF = ml_dtypes.bfloat16
def setup_inputs(rng):
    def f(*shape):
        return mx_ref.flush((rng.standard_normal(shape, dtype=np.float32) * np.exp2(rng.integers(-2, 3, shape[:-1] + (1,)))).astype(BF))
    return {"x": f(N, 128, 512), "rt": f(N, 128, 512), "w": f(N, 128, 4 * NC)}
def setup_inputs_blocks(rng):
    d = setup_inputs(rng)
    for k in ("x", "rt", "w"): d[k] = mx_ref.spread(d[k], rng, 4)
    return d
def setup_inputs_wide(rng):
    d = setup_inputs(rng)
    for k in ("x", "rt", "w"): d[k] = mx_ref.flush((d[k].astype(np.float32) * np.exp2(rng.integers(-6, 7, (N, 1, 1))).astype(np.float32)).astype(BF))
    return d
def setup_inputs_near(rng):
    d = setup_inputs(rng); v = d["rt"].astype(np.float32).reshape(N, 128, -1, 4)
    d["rt"] = mx_ref.flush((v[:, :, :1] + v / 64).reshape(d["rt"].shape).astype(BF))
    return d
def setup_inputs_twins(rng):
    d = setup_inputs(rng); v = d["rt"].reshape(N, 128, -1, 4).copy()
    v[:, :, 1] = v[:, :, 0]
    d["rt"] = v.reshape(d["rt"].shape)
    return d
def reference(x, rt, w):
    W = [mx_ref.quantize(w[e]) for e in range(N)]
    y = np.zeros((N, 128, NC), np.float32)
    for j in range(N):
        X = mx_ref.quantize(x[j])
        lg = mx_ref.matmul(X, mx_ref.quantize(rt[j]))[:, :N]
        m = lg.max(axis=1, keepdims=True)
        for e in range(N):
            y[j] = y[j] + (lg[:, e:e + 1] == m) * (mx_ref.matmul(X, W[e]) * m)
    return {"y": y}

@@ -1,0 +1,174 @@
+from concourse.bass import DstId, RemoteDMATransfer
+from concourse.mybir import dt, AluOpType, AxisListType, ActivationFunctionType
+
+N = 7
+NC = 128
+BANK = 512
+
+SCRATCH = {
+    "wb": ("sbuf", [128, 4 * NC], "bfloat16"),
+    "xb": ("sbuf", [128, 4 * NC], "bfloat16"),
+    "rb": ("sbuf", [128, 4 * NC], "bfloat16"),
+    "wq": ("sbuf", [128, N * NC], "float8_e4m3fn_x4"),
+    "ws": ("sbuf", [128, N * NC], "uint8"),
+    "xq": ("sbuf", [128, NC], "float8_e4m3fn_x4"),
+    "xs": ("sbuf", [128, NC], "uint8"),
+    "rq": ("sbuf", [128, NC], "float8_e4m3fn_x4"),
+    "rs": ("sbuf", [128, NC], "uint8"),
+    "ps": ("psum", [128, (N + 1) * BANK], "float32"),
+    "m": ("sbuf", [128, 4], "float32"),
+    "c": ("sbuf", [128, 8], "float32"),
+    "tmp": ("sbuf", [128, N * NC], "float32"),
+    "acc": ("sbuf", [128, NC], "float32"),
+}
+SEMAPHORES = (["ldw", "ldx", "ldr", "qw", "qx", "qr", "mml", "vm", "vc", "va", "st", "sent", "hc", "hp"]
+              + ["arr%d" % e for e in range(N)] + ["mm%d" % e for e in range(N)] + ["sc%d" % e for e in range(N)])
+
+
+def _bits(mask):
+    return bin(mask).count("1")
+
+
+def _plan(cores, topo):
+    every = range(topo.CHIPS * topo.CORES_PER_CHIP)
+    plan = {}
+    for r, c in enumerate(cores):
+        near = [q for q in range(len(cores)) if q == r or topo.may_write(c, cores[q])]
+        i = near.index(r)
+        direct = [near[(i + k) % len(near)] for k in range(1, len(near))]
+        far = [q for q in range(len(cores)) if q not in near]
+        far.sort(key=lambda q: topo.mates(topo.chip(c), topo.chip(cores[q])))
+        cand = [h for h in every if topo.chip(h) == topo.chip(c) and h not in cores
+                and all(topo.may_write(h, cores[q]) for q in far)]
+        same = [h for h in cand if topo.die(h) == topo.die(c)]
+        other = [h for h in cand if topo.die(h) != topo.die(c)]
+        a, b = (other, same) if i % 2 == 0 else (same, other)
+        turn = []
+        for k in range(max(len(a), len(b))):
+            turn += a[k:k + 1] + b[k:k + 1]
+        relays = []
+        for k in range((len(far) + 1) // 2):
+            part = far[2 * k:2 * k + 2]
+            rot = i % len(part)
+            relays.append((turn[k], part[rot:] + part[:rot]))
+        groups = [[x for x in relays if len(x[1]) == 2], [x for x in relays if len(x[1]) == 1]]
+        off = [q for q in range(len(cores)) if topo.chip(cores[q]) != topo.chip(c)][0]
+        lo = topo.mask(c, cores[off])
+        hi = topo.mask(c, relays[0][0]) & ~lo
+        plan[r] = {"direct": direct, "groups": [x for x in groups if x], "lo": lo, "hi": hi}
+    return plan
+
+
+def _order(plan, d):
+    score = {}
+    for r, p in plan.items():
+        if d in p["direct"]:
+            score[r] = (0, 0, p["direct"].index(d))
+        for k, grp in enumerate(p["groups"]):
+            for _h, part in grp:
+                if d in part:
+                    score[r] = (1, part.index(d), k)
+    return sorted(score, key=lambda r: score[r])
+
+
+def _send(g, T, topo, codes, slot, dsts, mask, sem):
+    def view():
+        if codes:
+            return T.wq[:, slot * NC:(slot + 1) * NC].bitcast(dt.uint8)
+        return T.ws[:, slot * NC:(slot + 1) * NC]
+    ids = [DstId(rid=topo.addr(d)[0], pnc=topo.addr(d)[1]) for d in dsts]
+    g.remote_dma_fused([RemoteDMATransfer(dst_ids=ids, dma_engine_mask=mask, remote_sem=sem,
+                                          srcs=[view()], dsts=[view() for _ in dsts])], local_sem=T.sem.sent)
+    return _bits(mask)
+
+
+def _relay(g, core, T, topo, cores, r, part, p):
+    dsts = [cores[q] for q in part]
+    mask = topo.mask(core, dsts[0])
+    for d in dsts:
+        mask &= topo.mask(core, d)
+    arr = T.sem["arr%d" % r]
+    g.wait_ge(T.sem.hp, _bits(p["lo"]))
+    n = _send(g, T, topo, False, r, dsts, mask, arr)
+    g.wait_ge(T.sem.hc, _bits(p["hi"]))
+    n += _send(g, T, topo, True, r, dsts, mask, arr)
+    g.wait_ge(T.sem.sent, n)
+
+
+def rank_program(g, core, T, topo):
+    cores = [int(c) for c in T.cores]
+    plan = _plan(cores, topo)
+    rank = T.rank_of(core)
+    if rank is None:
+        for r, p in plan.items():
+            for grp in p["groups"]:
+                for h, part in grp:
+                    if h == core:
+                        _relay(g, core, T, topo, cores, r, part, p)
+        return
+    p = plan[rank]
+    S = T.sem
+    own = slice(rank * NC, (rank + 1) * NC)
+
+    g.sync.dma_start(T.wb[:], T.w[:]).then_inc(S.ldw, 16)
+    g.sync.dma_start(T.xb[:], T.x[:]).then_inc(S.ldx, 16)
+    g.sync.dma_start(T.rb[:], T.rt[:]).then_inc(S.ldr, 16)
+
+    v = g.vector
+    v.wait_ge(S.ldw, 16)
+    v.quantize_mx(T.wq[:, own], T.ws[:, own], T.wb[:]).then_inc(S.qw, 1)
+    v.wait_ge(S.ldx, 16)
+    v.quantize_mx(T.xq[:], T.xs[:], T.xb[:]).then_inc(S.qx, 1)
+    v.wait_ge(S.ldr, 16)
+    v.quantize_mx(T.rq[:], T.rs[:], T.rb[:]).then_inc(S.qr, 1)
+
+    g.wait_ge(S.qw, 1)
+    n = 0
+    for grp in p["groups"]:
+        hs = [h for h, _part in grp]
+        n += _send(g, T, topo, True, rank, hs, p["hi"], S.hc)
+        n += _send(g, T, topo, False, rank, hs, p["lo"], S.hp)
+    ds = [cores[q] for q in p["direct"]]
+    arr = S["arr%d" % rank]
+    n += _send(g, T, topo, True, rank, ds, p["lo"], arr)
+    n += _send(g, T, topo, False, rank, ds, p["lo"], arr)
+
+    order = _order(plan, rank)
+    t = g.tensor
+    L = T.ps[:, N * BANK:N * BANK + NC]
+    t.wait_ge(S.qx, 1)
+    t.wait_ge(S.qr, 1)
+    t.matmul_mx(L, T.xq[:], T.xs[:], T.rq[:], T.rs[:], True, True).then_inc(S.mml, 1)
+    t.wait_ge(S.qw, 1)
+    for e in [rank] + order:
+        if e != rank:
+            t.wait_ge(S["arr%d" % e], 2 * _bits(plan[e]["lo"]))
+        sl = slice(e * NC, (e + 1) * NC)
+        t.matmul_mx(T.ps[:, e * BANK:e * BANK + NC], T.xq[:], T.xs[:], T.wq[:, sl], T.ws[:, sl],
+                    True, True).then_inc(S["mm%d" % e], 1)
+
+    lg = T.ps[:, N * BANK:N * BANK + N]
+    v.wait_ge(S.mml, 1)
+    v.tensor_reduce(T.m[:, 0:1], lg, AxisListType.X, AluOpType.max).then_inc(S.vm, 1)
+    v.wait_ge(S.vm, 1)
+    v.tensor_scalar(T.c[:, 0:N], lg, T.m[:, 0:1], T.m[:, 0:1], AluOpType.is_equal, AluOpType.mult).then_inc(S.vc, 1)
+    v.wait_ge(S.vc, 1)
+    v.wait_ge(S["mm%d" % rank], 1)
+    v.tensor_scalar(T.acc[:], T.ps[:, rank * BANK:rank * BANK + NC], T.c[:, rank:rank + 1], 0.0,
+                    AluOpType.mult, AluOpType.add).then_inc(S.va, 1)
+
+    s = g.scalar
+    s.wait_ge(S.vc, 1)
+    for k, e in enumerate(order):
+        sl = slice(e * NC, (e + 1) * NC)
+        s.wait_ge(S["mm%d" % e], 1)
+        s.activation(T.tmp[:, sl], T.ps[:, e * BANK:e * BANK + NC], ActivationFunctionType.Copy,
+                     scale=T.c[:, e:e + 1]).then_inc(S["sc%d" % e], 1)
+        v.wait_ge(S["sc%d" % e], 1)
+        v.wait_ge(S.va, k + 1)
+        v.tensor_tensor(T.acc[:], T.acc[:], T.tmp[:, sl], AluOpType.add).then_inc(S.va, 1)
+
+    g.sync.wait_ge(S.va, N)
+    g.sync.dma_start(T.y[:], T.acc[:]).then_inc(S.st, 16)
+    g.sync.wait_ge(S.st, 16)
+    g.wait_ge(S.sent, n)

@@ -4,6 +4,7 @@ from concourse.mybir import dt, AluOpType, AxisListType, ActivationFunctionType
 N = 7
 NC = 128
 BANK = 512
+DIRECT = 3
 
 SCRATCH = {
     "wb": ("sbuf", [128, 4 * NC], "bfloat16"),
@@ -21,7 +22,7 @@ SCRATCH = {
     "tmp": ("sbuf", [128, N * NC], "float32"),
     "acc": ("sbuf", [128, NC], "float32"),
 }
-SEMAPHORES = (["ldw", "ldx", "ldr", "qw", "qx", "qr", "mml", "vm", "vc", "va", "st", "sent", "hc", "hp"]
+SEMAPHORES = (["ldw", "ldx", "ldr", "qw", "qx", "qr", "mml", "vm", "vc", "va", "st", "sent", "hp"]
               + ["arr%d" % e for e in range(N)] + ["mm%d" % e for e in range(N)] + ["sc%d" % e for e in range(N)])
 
 
@@ -35,27 +36,38 @@ def _plan(cores, topo):
     for r, c in enumerate(cores):
         near = [q for q in range(len(cores)) if q == r or topo.may_write(c, cores[q])]
         i = near.index(r)
-        direct = [near[(i + k) % len(near)] for k in range(1, len(near))]
+        reach = [near[(i + k) % len(near)] for k in range(1, len(near))]
+        direct, extra = reach[:DIRECT], reach[DIRECT:]
         far = [q for q in range(len(cores)) if q not in near]
-        far.sort(key=lambda q: topo.mates(topo.chip(c), topo.chip(cores[q])))
-        cand = [h for h in every if topo.chip(h) == topo.chip(c) and h not in cores
-                and all(topo.may_write(h, cores[q]) for q in far)]
-        same = [h for h in cand if topo.die(h) == topo.die(c)]
-        other = [h for h in cand if topo.die(h) != topo.die(c)]
+        home = [h for h in every if topo.chip(h) == topo.chip(c) and h not in cores]
+        port = [h for h in home if all(topo.may_write(h, cores[q]) for q in far)]
+        s = (2 * i if len(far) > len(port) else i // 2) % len(far)
+        far = far[s:] + far[:s]
+        same = [h for h in port if topo.die(h) == topo.die(c)]
+        other = [h for h in port if topo.die(h) != topo.die(c)]
         a, b = (other, same) if i % 2 == 0 else (same, other)
         turn = []
         for k in range(max(len(a), len(b))):
             turn += a[k:k + 1] + b[k:k + 1]
-        relays = []
-        for k in range((len(far) + 1) // 2):
-            part = far[2 * k:2 * k + 2]
-            rot = i % len(part)
-            relays.append((turn[k], part[rot:] + part[:rot]))
-        groups = [[x for x in relays if len(x[1]) == 2], [x for x in relays if len(x[1]) == 1]]
+        relays = [(turn[k], q) for k, q in enumerate(far[:len(turn)])]
+        shared = far[len(turn):]
+        half, xplane = {}, None
+        if shared:
+            half = {relays[0][0]: 0, relays[1][0]: 1}
+            xplane = relays[2][0]
+        spare = [h for h in home if h not in port and topo.die(h) != topo.die(c)]
+        for k, q in enumerate(extra):
+            relays.append((spare[k], q))
         off = [q for q in range(len(cores)) if topo.chip(cores[q]) != topo.chip(c)][0]
         lo = topo.mask(c, cores[off])
         hi = topo.mask(c, relays[0][0]) & ~lo
-        plan[r] = {"direct": direct, "groups": [x for x in groups if x], "lo": lo, "hi": hi}
+        hi_d = [h for h, _q in relays]
+        lo_d = [cores[q] for q in direct]
+        while len(hi_d) > len(lo_d) + 1:
+            lo_d = [hi_d[-1]] + lo_d
+            hi_d = hi_d[:-1]
+        plan[r] = {"direct": direct, "relays": relays, "shared": shared, "half": half, "xplane": xplane,
+                   "lo": lo, "hi": hi, "hi_d": hi_d, "lo_d": lo_d}
     return plan
 
 
@@ -63,35 +75,39 @@ def _order(plan, d):
     score = {}
     for r, p in plan.items():
         if d in p["direct"]:
-            score[r] = (0, 0, p["direct"].index(d))
-        for k, grp in enumerate(p["groups"]):
-            for _h, part in grp:
-                if d in part:
-                    score[r] = (1, part.index(d), k)
-    return sorted(score, key=lambda r: score[r])
+            score[r] = 10 * p["direct"].index(d)
+        for k, (_h, q) in enumerate(p["relays"]):
+            if q == d:
+                score[r] = 15 + 3 * k
+        if d in p["shared"]:
+            score[r] = 35
+    return sorted(score, key=lambda r: (score[r], r))
 
 
-def _send(g, T, topo, codes, slot, dsts, mask, sem):
+def _tr(T, topo, codes, slot, dsts, mask, sem, a=0, b=NC):
     def view():
         if codes:
-            return T.wq[:, slot * NC:(slot + 1) * NC].bitcast(dt.uint8)
-        return T.ws[:, slot * NC:(slot + 1) * NC]
+            return T.wq[:, slot * NC + a:slot * NC + b].bitcast(dt.uint8)
+        return T.ws[:, slot * NC + a:slot * NC + b]
     ids = [DstId(rid=topo.addr(d)[0], pnc=topo.addr(d)[1]) for d in dsts]
-    g.remote_dma_fused([RemoteDMATransfer(dst_ids=ids, dma_engine_mask=mask, remote_sem=sem,
-                                          srcs=[view()], dsts=[view() for _ in dsts])], local_sem=T.sem.sent)
-    return _bits(mask)
+    return RemoteDMATransfer(dst_ids=ids, dma_engine_mask=mask, remote_sem=sem,
+                             srcs=[view()], dsts=[view() for _ in dsts])
 
 
-def _relay(g, core, T, topo, cores, r, part, p):
-    dsts = [cores[q] for q in part]
-    mask = topo.mask(core, dsts[0])
-    for d in dsts:
-        mask &= topo.mask(core, d)
+def _relay(g, core, T, topo, cores, r, q, p):
+    mask = topo.mask(core, cores[q])
     arr = T.sem["arr%d" % r]
-    g.wait_ge(T.sem.hp, _bits(p["lo"]))
-    n = _send(g, T, topo, False, r, dsts, mask, arr)
-    g.wait_ge(T.sem.hc, _bits(p["hi"]))
-    n += _send(g, T, topo, True, r, dsts, mask, arr)
+    pd = [cores[q]] + ([cores[z] for z in p["shared"]] if core == p["xplane"] else [])
+    g.wait_ge(T.sem.hp, _bits(p["hi"]))
+    g.remote_dma_fused([_tr(T, topo, False, r, pd, mask, arr)], local_sem=T.sem.sent)
+    g.wait_ge(arr, _bits(p["hi"] if core in p["hi_d"] else p["lo"]))
+    g.remote_dma_fused([_tr(T, topo, True, r, [cores[q]], mask, arr)], local_sem=T.sem.sent)
+    n = 2 * _bits(mask)
+    if core in p["half"]:
+        k = p["half"][core]
+        g.remote_dma_fused([_tr(T, topo, True, r, [cores[z] for z in p["shared"]], mask, arr,
+                                k * NC // 2, (k + 1) * NC // 2)], local_sem=T.sem.sent)
+        n += _bits(mask)
     g.wait_ge(T.sem.sent, n)
 
 
@@ -101,10 +117,9 @@ def rank_program(g, core, T, topo):
     rank = T.rank_of(core)
     if rank is None:
         for r, p in plan.items():
-            for grp in p["groups"]:
-                for h, part in grp:
-                    if h == core:
-                        _relay(g, core, T, topo, cores, r, part, p)
+            for h, q in p["relays"]:
+                if h == core:
+                    _relay(g, core, T, topo, cores, r, q, p)
         return
     p = plan[rank]
     S = T.sem
@@ -122,16 +137,13 @@ def rank_program(g, core, T, topo):
     v.wait_ge(S.ldr, 16)
     v.quantize_mx(T.rq[:], T.rs[:], T.rb[:]).then_inc(S.qr, 1)
 
-    g.wait_ge(S.qw, 1)
-    n = 0
-    for grp in p["groups"]:
-        hs = [h for h, _part in grp]
-        n += _send(g, T, topo, True, rank, hs, p["hi"], S.hc)
-        n += _send(g, T, topo, False, rank, hs, p["lo"], S.hp)
-    ds = [cores[q] for q in p["direct"]]
     arr = S["arr%d" % rank]
-    n += _send(g, T, topo, True, rank, ds, p["lo"], arr)
-    n += _send(g, T, topo, False, rank, ds, p["lo"], arr)
+    g.wait_ge(S.qw, 1)
+    g.remote_dma_fused([_tr(T, topo, False, rank, [h for h, _q in p["relays"]], p["hi"], S.hp)], local_sem=S.sent)
+    g.remote_dma_fused([_tr(T, topo, False, rank, [cores[q] for q in p["direct"]], p["lo"], arr)], local_sem=S.sent)
+    g.remote_dma_fused([_tr(T, topo, True, rank, p["hi_d"], p["hi"], arr),
+                        _tr(T, topo, True, rank, p["lo_d"], p["lo"], arr)], local_sem=S.sent)
+    n = 2 * _bits(p["hi"]) + 2 * _bits(p["lo"])
 
     order = _order(plan, rank)
     t = g.tensor
@@ -142,7 +154,8 @@ def rank_program(g, core, T, topo):
     t.wait_ge(S.qw, 1)
     for e in [rank] + order:
         if e != rank:
-            t.wait_ge(S["arr%d" % e], 2 * _bits(plan[e]["lo"]))
+            pieces = 3 if rank in plan[e]["shared"] else 2
+            t.wait_ge(S["arr%d" % e], pieces * _bits(plan[e]["lo"]))
         sl = slice(e * NC, (e + 1) * NC)
         t.matmul_mx(T.ps[:, e * BANK:e * BANK + NC], T.xq[:], T.xs[:], T.wq[:, sl], T.ws[:, sl],
                     True, True).then_inc(S["mm%d" % e], 1)

from concourse.bass import DstId, RemoteDMATransfer
from concourse.mybir import dt, AluOpType, AxisListType, ActivationFunctionType

N = 7
NC = 128
BANK = 512
DIRECT = 3

SCRATCH = {
    "wb": ("sbuf", [128, 4 * NC], "bfloat16"),
    "xb": ("sbuf", [128, 4 * NC], "bfloat16"),
    "rb": ("sbuf", [128, 4 * NC], "bfloat16"),
    "wq": ("sbuf", [128, N * NC], "float8_e4m3fn_x4"),
    "ws": ("sbuf", [128, N * NC], "uint8"),
    "xq": ("sbuf", [128, NC], "float8_e4m3fn_x4"),
    "xs": ("sbuf", [128, NC], "uint8"),
    "rq": ("sbuf", [128, NC], "float8_e4m3fn_x4"),
    "rs": ("sbuf", [128, NC], "uint8"),
    "ps": ("psum", [128, (N + 1) * BANK], "float32"),
    "m": ("sbuf", [128, 4], "float32"),
    "c": ("sbuf", [128, 8], "float32"),
    "tmp": ("sbuf", [128, N * NC], "float32"),
    "acc": ("sbuf", [128, NC], "float32"),
}
SEMAPHORES = (["ldw", "ldx", "ldr", "qw", "qx", "qr", "mml", "vm", "vc", "va", "st", "sent", "hp"]
              + ["arr%d" % e for e in range(N)] + ["mm%d" % e for e in range(N)] + ["sc%d" % e for e in range(N)])


def _bits(mask):
    return bin(mask).count("1")


def _plan(cores, topo):
    every = range(topo.CHIPS * topo.CORES_PER_CHIP)
    plan = {}
    for r, c in enumerate(cores):
        near = [q for q in range(len(cores)) if q == r or topo.may_write(c, cores[q])]
        i = near.index(r)
        reach = [near[(i + k) % len(near)] for k in range(1, len(near))]
        direct, extra = reach[:DIRECT], reach[DIRECT:]
        far = [q for q in range(len(cores)) if q not in near]
        home = [h for h in every if topo.chip(h) == topo.chip(c) and h not in cores]
        port = [h for h in home if all(topo.may_write(h, cores[q]) for q in far)]
        s = (2 * i if len(far) > len(port) else i // 2) % len(far)
        far = far[s:] + far[:s]
        same = [h for h in port if topo.die(h) == topo.die(c)]
        other = [h for h in port if topo.die(h) != topo.die(c)]
        a, b = (other, same) if i % 2 == 0 else (same, other)
        turn = []
        for k in range(max(len(a), len(b))):
            turn += a[k:k + 1] + b[k:k + 1]
        relays = [(turn[k], q) for k, q in enumerate(far[:len(turn)])]
        shared = far[len(turn):]
        half, xplane = {}, None
        if shared:
            half = {relays[0][0]: 0, relays[1][0]: 1}
            xplane = relays[2][0]
        spare = [h for h in home if h not in port and topo.die(h) != topo.die(c)]
        for k, q in enumerate(extra):
            relays.append((spare[k], q))
        off = [q for q in range(len(cores)) if topo.chip(cores[q]) != topo.chip(c)][0]
        lo = topo.mask(c, cores[off])
        hi = topo.mask(c, relays[0][0]) & ~lo
        hi_d = [h for h, _q in relays]
        lo_d = [cores[q] for q in direct]
        while len(hi_d) > len(lo_d) + 1:
            lo_d = [hi_d[-1]] + lo_d
            hi_d = hi_d[:-1]
        plan[r] = {"direct": direct, "relays": relays, "shared": shared, "half": half, "xplane": xplane,
                   "lo": lo, "hi": hi, "hi_d": hi_d, "lo_d": lo_d}
    return plan


def _order(plan, d):
    score = {}
    for r, p in plan.items():
        if d in p["direct"]:
            score[r] = 10 * p["direct"].index(d)
        for k, (_h, q) in enumerate(p["relays"]):
            if q == d:
                score[r] = 15 + 3 * k
        if d in p["shared"]:
            score[r] = 35
    return sorted(score, key=lambda r: (score[r], r))


def _tr(T, topo, codes, slot, dsts, mask, sem, a=0, b=NC):
    def view():
        if codes:
            return T.wq[:, slot * NC + a:slot * NC + b].bitcast(dt.uint8)
        return T.ws[:, slot * NC + a:slot * NC + b]
    ids = [DstId(rid=topo.addr(d)[0], pnc=topo.addr(d)[1]) for d in dsts]
    return RemoteDMATransfer(dst_ids=ids, dma_engine_mask=mask, remote_sem=sem,
                             srcs=[view()], dsts=[view() for _ in dsts])


def _relay(g, core, T, topo, cores, r, q, p):
    mask = topo.mask(core, cores[q])
    arr = T.sem["arr%d" % r]
    pd = [cores[q]] + ([cores[z] for z in p["shared"]] if core == p["xplane"] else [])
    g.wait_ge(T.sem.hp, _bits(p["hi"]))
    g.remote_dma_fused([_tr(T, topo, False, r, pd, mask, arr)], local_sem=T.sem.sent)
    g.wait_ge(arr, _bits(p["hi"] if core in p["hi_d"] else p["lo"]))
    g.remote_dma_fused([_tr(T, topo, True, r, [cores[q]], mask, arr)], local_sem=T.sem.sent)
    n = 2 * _bits(mask)
    if core in p["half"]:
        k = p["half"][core]
        g.remote_dma_fused([_tr(T, topo, True, r, [cores[z] for z in p["shared"]], mask, arr,
                                k * NC // 2, (k + 1) * NC // 2)], local_sem=T.sem.sent)
        n += _bits(mask)
    g.wait_ge(T.sem.sent, n)


def rank_program(g, core, T, topo):
    cores = [int(c) for c in T.cores]
    plan = _plan(cores, topo)
    rank = T.rank_of(core)
    if rank is None:
        for r, p in plan.items():
            for h, q in p["relays"]:
                if h == core:
                    _relay(g, core, T, topo, cores, r, q, p)
        return
    p = plan[rank]
    S = T.sem
    own = slice(rank * NC, (rank + 1) * NC)

    g.sync.dma_start(T.wb[:], T.w[:]).then_inc(S.ldw, 16)
    g.sync.dma_start(T.xb[:], T.x[:]).then_inc(S.ldx, 16)
    g.sync.dma_start(T.rb[:], T.rt[:]).then_inc(S.ldr, 16)

    v = g.vector
    v.wait_ge(S.ldw, 16)
    v.quantize_mx(T.wq[:, own], T.ws[:, own], T.wb[:]).then_inc(S.qw, 1)
    v.wait_ge(S.ldx, 16)
    v.quantize_mx(T.xq[:], T.xs[:], T.xb[:]).then_inc(S.qx, 1)
    v.wait_ge(S.ldr, 16)
    v.quantize_mx(T.rq[:], T.rs[:], T.rb[:]).then_inc(S.qr, 1)

    arr = S["arr%d" % rank]
    g.wait_ge(S.qw, 1)
    g.remote_dma_fused([_tr(T, topo, False, rank, [h for h, _q in p["relays"]], p["hi"], S.hp)], local_sem=S.sent)
    g.remote_dma_fused([_tr(T, topo, False, rank, [cores[q] for q in p["direct"]], p["lo"], arr)], local_sem=S.sent)
    g.remote_dma_fused([_tr(T, topo, True, rank, p["hi_d"], p["hi"], arr),
                        _tr(T, topo, True, rank, p["lo_d"], p["lo"], arr)], local_sem=S.sent)
    n = 2 * _bits(p["hi"]) + 2 * _bits(p["lo"])

    order = _order(plan, rank)
    t = g.tensor
    L = T.ps[:, N * BANK:N * BANK + NC]
    t.wait_ge(S.qx, 1)
    t.wait_ge(S.qr, 1)
    t.matmul_mx(L, T.xq[:], T.xs[:], T.rq[:], T.rs[:], True, True).then_inc(S.mml, 1)
    t.wait_ge(S.qw, 1)
    for e in [rank] + order:
        if e != rank:
            pieces = 3 if rank in plan[e]["shared"] else 2
            t.wait_ge(S["arr%d" % e], pieces * _bits(plan[e]["lo"]))
        sl = slice(e * NC, (e + 1) * NC)
        t.matmul_mx(T.ps[:, e * BANK:e * BANK + NC], T.xq[:], T.xs[:], T.wq[:, sl], T.ws[:, sl],
                    True, True).then_inc(S["mm%d" % e], 1)

    lg = T.ps[:, N * BANK:N * BANK + N]
    v.wait_ge(S.mml, 1)
    v.tensor_reduce(T.m[:, 0:1], lg, AxisListType.X, AluOpType.max).then_inc(S.vm, 1)
    v.wait_ge(S.vm, 1)
    v.tensor_scalar(T.c[:, 0:N], lg, T.m[:, 0:1], T.m[:, 0:1], AluOpType.is_equal, AluOpType.mult).then_inc(S.vc, 1)
    v.wait_ge(S.vc, 1)
    v.wait_ge(S["mm%d" % rank], 1)
    v.tensor_scalar(T.acc[:], T.ps[:, rank * BANK:rank * BANK + NC], T.c[:, rank:rank + 1], 0.0,
                    AluOpType.mult, AluOpType.add).then_inc(S.va, 1)

    s = g.scalar
    s.wait_ge(S.vc, 1)
    for k, e in enumerate(order):
        sl = slice(e * NC, (e + 1) * NC)
        s.wait_ge(S["mm%d" % e], 1)
        s.activation(T.tmp[:, sl], T.ps[:, e * BANK:e * BANK + NC], ActivationFunctionType.Copy,
                     scale=T.c[:, e:e + 1]).then_inc(S["sc%d" % e], 1)
        v.wait_ge(S["sc%d" % e], 1)
        v.wait_ge(S.va, k + 1)
        v.tensor_tensor(T.acc[:], T.acc[:], T.tmp[:, sl], AluOpType.add).then_inc(S.va, 1)

    g.sync.wait_ge(S.va, N)
    g.sync.dma_start(T.y[:], T.acc[:]).then_inc(S.st, 16)
    g.sync.wait_ge(S.st, 16)
    g.wait_ge(S.sent, n)
